import numpy as np
import ml_dtypes


def mxq(x, axis, fmt="e4m3"):
    dtype, down = {"e4m3": (ml_dtypes.float8_e4m3fn, 7), "e5m2": (ml_dtypes.float8_e5m2, 14)}[fmt]
    v = np.moveaxis(np.asarray(x, np.float32).astype(ml_dtypes.bfloat16).astype(np.float64), axis, -1)
    blocks = v.reshape(v.shape[:-1] + (-1, 32))
    amax = np.abs(blocks).max(-1, keepdims=True)
    byte = np.maximum(np.where(amax > 0, np.frexp(amax)[1] - 1 + 127, 0) - down, 1)
    scale = np.exp2(byte - 127.0)
    codes = (blocks / scale).astype(np.float32).astype(dtype).astype(np.float64)
    return np.moveaxis((codes * scale).reshape(v.shape), -1, axis)


WIDE = False


def mx_kscale(k):
    if not WIDE:
        return np.ones(k)
    levels = np.array([10, -10, 5, -5, 0])
    if k % 512:
        return np.exp2(np.random.permutation(np.resize(levels, k // 32))).repeat(32)
    a = np.empty((k // 512, 16))
    for p in range(k // 512):
        a[p, :8] = np.random.permutation(np.resize(levels, 8))
        for g in range(8):
            far = levels[np.abs(levels - a[p, g]) >= 10]
            a[p, g + 8] = far[np.random.randint(len(far))]
    return np.exp2(a.ravel()).repeat(32)


def f64(x):
    return np.asarray(x).astype(np.float64)


def striped(idx):
    return np.tile(idx.reshape(-1, 16).T, (8, 1)).astype(np.uint16)


def unstriped(offs):
    return offs[:16].T.reshape(-1).astype(np.int64)


E2M1 = np.array([0.0, 0.5, 1.0, 1.5, 2.0, 3.0, 4.0, 6.0, -0.0, -0.5, -1.0, -1.5, -2.0, -3.0, -4.0, -6.0])


def pack_weight(w, fmt):
    k, n = w.shape
    w = f64(np.asarray(w, np.float32).astype(ml_dtypes.bfloat16)).reshape(k // 32, 32, n)
    amax = np.abs(w).max(1)
    if fmt == "e4m3":
        byte = np.frexp(amax)[1] - 1 + 127 - 7
    else:
        mant, ex = np.frexp(amax / 6.0)
        byte = np.where(mant > 0.5, ex, ex - 1) + 127
    byte = np.clip(np.where(amax > 0, byte, 1), 1, 254)
    scaled = (w * np.exp2(127.0 - byte)[:, None, :]).reshape(k, n).astype(np.float32)
    by_word = np.ascontiguousarray(scaled.reshape(k // 512, 128, 4, n).transpose(0, 1, 3, 2))
    if fmt == "e4m3":
        words = by_word.astype(ml_dtypes.float8_e4m3fn).view(np.uint8)
    else:
        c = by_word.astype(ml_dtypes.float4_e2m1fn).view(np.uint8) & 0xF
        words = (c[..., 0::2] | (c[..., 1::2] << 4)).reshape(k // 512, 128, 2 * n)
    return np.ascontiguousarray(words), np.ascontiguousarray(byte.astype(np.uint8).reshape(k // 512, 16, n))


def unpack_weight(words, scales, fmt):
    g, _, n = scales.shape
    words = np.ascontiguousarray(words).reshape(g, 128, n, -1)
    if fmt == "e4m3":
        vals = words.view(ml_dtypes.float8_e4m3fn).astype(np.float64)
    else:
        nib = np.empty((g, 128, n, 4), np.uint8)
        nib[..., 0::2] = words & 0xF
        nib[..., 1::2] = words >> 4
        vals = E2M1[nib]
    vals = vals * np.repeat(np.exp2(scales.astype(np.float64) - 127.0), 8, axis=1)[..., None]
    return vals.transpose(0, 1, 3, 2).reshape(g * 512, n)


def gelu(v):
    return 0.5 * v * (1.0 + np.tanh(np.sqrt(2.0 / np.pi) * (v + 0.044715 * v**3)))


def bf(x):
    return np.asarray(x, np.float32).astype(ml_dtypes.bfloat16)


def planes(Y):
    n, m = Y.shape
    b = f64(bf(Y)).reshape(n // 32, 32, m)
    amax = np.abs(b).max(1)
    byte = np.clip(np.where(amax > 0, np.frexp(amax)[1] - 1 + 127 - 7, 1), 1, 254)
    codes = (b * np.exp2(127.0 - byte)[:, None, :]).reshape(n, m).astype(np.float32).astype(ml_dtypes.float8_e4m3fn).view(np.uint8)
    words = codes.reshape(n // 512, 128, 4, m).transpose(0, 1, 3, 2)
    return np.ascontiguousarray(words), np.ascontiguousarray(byte.astype(np.uint8).reshape(n // 512, 16, m))


K, H, N, T, S = 1024, 512, 768, 2048, 1024

def setup_inputs():
    n = np.random.standard_normal
    s = mx_kscale(K)[:, None]
    u = mx_kscale(H)[:, None]
    tab_words, tab_scales = pack_weight(n((K, T)) * s, "e4m3")
    w1_words, w1_scales = pack_weight(n((K, H)) / np.sqrt(K) / s * u.T, "e2m1")
    w3_words, w3_scales = pack_weight(n((K, H)) / np.sqrt(K) / s * u.T, "e4m3")
    return {
        "tab_words": tab_words, "tab_scales": tab_scales,
        "offs": striped(np.random.permutation(T)[:S]),
        "w1_words": w1_words, "w1_scales": w1_scales,
        "w2": (n((K, H)) / np.sqrt(K) / s).astype(np.float32),
        "w3_words": w3_words, "w3_scales": w3_scales,
        "w4": (n((H, N)) / np.sqrt(H) / u).astype(np.float32),
        "w5": (n((K, N)) / np.sqrt(K) / s).astype(np.float32),
        "b5": (0.5 * n(N)).astype(np.float32),
    }

def reference(tab_words, tab_scales, offs, w1_words, w1_scales, w2,
              w3_words, w3_scales, w4, w5, b5):
    v = unpack_weight(tab_words, tab_scales, "e4m3")[:, unstriped(offs)]
    w1 = unpack_weight(w1_words, w1_scales, "e2m1")
    w3 = unpack_weight(w3_words, w3_scales, "e4m3")
    a = w1.T @ v
    b = mxq(f64(w2), 0, "e4m3").T @ v
    h = a * b + (w3.T @ v)
    e = (mxq(f64(w5), 0, "e4m3").T @ v) + f64(b5)[:, None]
    y = (mxq(f64(w4), 0, "e4m3").T @ mxq(h, 0, "e4m3")) - e / (1 + np.exp(-e))
    words, scales = planes(h)
    return y, h, words, scales

@@ -1,0 +1,329 @@
+from contextlib import ExitStack
+
+import concourse.mybir as mybir
+
+K, H, N, T, S = 1024, 512, 768, 2048, 1024
+FLOPS = 2 * S * (3 * K * H + K * N + H * N)
+
+F32 = mybir.dt.float32
+BF16 = mybir.dt.bfloat16
+I32 = mybir.dt.int32
+U32 = mybir.dt.uint32
+U16 = mybir.dt.uint16
+U8 = mybir.dt.uint8
+FP8X4 = mybir.dt.float8_e4m3fn_x4
+FP4X4 = mybir.dt.float4_e2m1fn_x4
+ALU = mybir.AluOpType
+ACT = mybir.ActivationFunctionType
+
+P = 128
+PACK = 4
+PASSES = K // (P * PACK)
+HALF = 512
+HALVES = S // HALF
+CHUNK = 256
+CHUNKS = N // CHUNK
+
+W5_ENGINES = (("s", "s", "s"), ("s", "s", "s"))
+W4_ENGINES = ("s", "s", "s")
+H_ENGINES = (("s","v"), ("s","v"))
+W2_ENGINES = (("v",), ("v",))
+
+
+def cast(nc, engine, out, in_):
+    if engine == "v":
+        nc.vector.tensor_copy(out=out, in_=in_)
+    elif engine == "s":
+        nc.scalar.copy(out=out, in_=in_)
+    else:
+        nc.gpsimd.tensor_scalar(out=out, in0=in_, scalar1=1.0, scalar2=0.0, op0=ALU.mult, op1=ALU.add)
+
+
+def interleave(nc, engine, grouped, rows):
+    if engine == "g":
+        cast(nc, engine, grouped, rows.rearrange("p j c -> p c j"))
+        return
+    cast(
+        nc,
+        engine,
+        grouped.rearrange("p (c i) j -> p c j i", i=4),
+        rows.rearrange("p j (c i) -> p c j i", i=4),
+    )
+
+
+def quantize(nc, codes, scales, grouped):
+    nc.vector.quantize_mx(out=codes.bitcast(FP8X4), scales=scales, in_=grouped)
+
+
+def tile_list_chirp_interference_repair_kernel(
+    tc, tab_words, tab_scales, offs, w1_words, w1_scales, w2, w3_words, w3_scales, w4, w5, b5,
+    out_0, out_1, out_2, out_3,
+):
+    nc = tc.nc
+    with ExitStack() as ctx:
+        keep = ctx.enter_context(tc.tile_pool(name="keep", bufs=1))
+        ring = ctx.enter_context(tc.tile_pool(name="ring", bufs=3))
+        psum = ctx.enter_context(tc.psum_pool(name="psum", bufs=2))
+
+        def held(shape, dtype, name, tag=""):
+            return keep.tile(shape, dtype, name=name, tag=tag or name, align_bytes=64)
+
+        offsets = keep.tile([P, S // 16], U16, name="offsets")
+        tab_planes = held([P, T], U8, "tab_planes")
+        v_planes = held([P, S], U8, "v_planes")
+        v_plane1 = held([P, S], U8, "v_plane1")
+        w_planes_raw = held([P, PASSES, H], U8, "w_planes_raw")
+        nc.vector.memset(tab_planes[:].bitcast(I32), 0)
+        nc.gpsimd.memset(w_planes_raw[:].bitcast(I32), 0)
+        w3_planes_raw = held([P, H], U8, "w3_planes_raw")
+        nc.gpsimd.memset(w3_planes_raw[:].bitcast(I32), 0)
+        nc.gpsimd.memset(v_plane1[:].bitcast(I32), 0)
+
+        warm = held([P, 8], F32, "warm")
+        nc.gpsimd.memset(warm[:, 0:1], 0.0)
+        nc.scalar.activation(out=warm[:, 1:2], in_=warm[:, 0:1], func=ACT.Silu)
+
+        w1_raw = held([P, PASSES, 2 * H], U8, "w1_raw")
+        tab = [held([P, T], I32, f"tab{a}") for a in range(PASSES)]
+
+        def load_rows(tile, w, a):
+            nc.sync.dma_start(out=tile[:], in_=w[512 * a : 512 * (a + 1), :].rearrange("(p j) c -> p j c", j=PACK))
+
+        def load_tab(a):
+            nc.sync.dma_start(out=tab[a][:], in_=tab_words[a].rearrange("p t i -> p (t i)").bitcast(I32))
+
+        def load_packed(tile, scales):
+            for q in range(4):
+                nc.sync.dma_start(
+                    out=tile[32 * q : 32 * q + 8, :].bitcast(I32), in_=scales[:, 4 * q : 4 * q + 4, :].bitcast(I32)
+                )
+
+        def load_planes(queue, tile, first, scales):
+            for q in range(4):
+                queue.dma_start(
+                    out=tile[32 * q + first : 32 * q + first + 4].bitcast(I32),
+                    in_=scales[:, 4 * q : 4 * q + 4, :].rearrange("a r c -> r a c").bitcast(I32),
+                )
+
+        nc.sync.dma_start(out=w1_raw[:].bitcast(I32), in_=w1_words.rearrange("a p c -> p a c").bitcast(I32))
+        nc.sync.dma_start(offsets[:], offs)
+        for q in range(4):
+            nc.sync.dma_start(
+                out=tab_planes[32 * q : 32 * q + 8, :].bitcast(I32),
+                in_=tab_scales[:, 4 * q : 4 * q + 4, :].bitcast(I32),
+            )
+        load_tab(0)
+        load_planes(nc.sync, w_planes_raw, 0, w1_scales)
+        load_tab(1)
+        load_packed(w3_planes_raw, w3_scales)
+
+        v_words = [[held([P, HALF], U32, f"v_words{a}{s}") for s in range(HALVES)] for a in range(PASSES)]
+
+        def picks(s):
+            return offsets[:, s * HALF // 16 : (s + 1) * HALF // 16]
+
+        def gather_words(a, s):
+            nc.vector.tensor_copy(v_words[a][s][:], tab[a][:].bitcast(U32).indirect(picks(s)))
+
+        def gather_planes():
+            nc.vector.tensor_copy(v_planes[:], tab_planes[:].indirect(offsets[:]))
+            nc.scalar.dma_start(out=v_plane1[0:100, :].bitcast(I32), in_=v_planes[4:104, :].bitcast(I32))
+
+        w1_codes = held([P, PASSES, 2 * H], U8, "w1_codes")
+        w3_codes = held([P, PASSES, H], I32, "w3_codes")
+        w_planes = held([P, PASSES, H], U8, "w_planes")
+
+        def deal(out, in_):
+            nc.vector.tensor_copy(
+                out=out.rearrange("p a (t m) -> p a m t", t=PACK), in_=in_.rearrange("p a (m t) -> p a m t", t=PACK)
+            )
+
+        w2_bf = [held([P, PACK, P, PACK], BF16, f"w2_bf{a}") for a in range(PASSES)]
+        w2_codes = [held([P, H], U32, f"w2_codes{a}") for a in range(PASSES)]
+        w2_planes = [held([P, H], U8, f"w2_planes{a}") for a in range(PASSES)]
+
+        def round_w2(a):
+            for part, engine in enumerate(W2_ENGINES[a]):
+                width = P // len(W2_ENGINES[a])
+                ms = slice(part * width, (part + 1) * width)
+                cast(
+                    nc,
+                    engine,
+                    w2_bf[a][:, :, ms, :].rearrange("p t m j -> p m j t"),
+                    w2_raw[a][:].rearrange("p j (m t) -> p m j t", t=PACK)[:, ms],
+                )
+
+        def quantize_w2(a):
+            quantize(nc, w2_codes[a][:], w2_planes[a][:], w2_bf[a][:].rearrange("p t m j -> p (t m j)"))
+
+        deal(w1_codes[:].bitcast(U16), w1_raw[:].bitcast(U16))
+        gather_planes()
+        gather_words(0, 0)
+        deal(w_planes[:], w_planes_raw[:])
+        gather_words(1, 0)
+        gather_words(0, 1)
+        gather_words(1, 1)
+        w2_raw = [held([P, PACK, H], F32, f"w2_raw{a}", ("tab_planes", "tab0")[a]) for a in range(PASSES)]
+        w3_raw = held([P, PASSES, H], I32, "w3_raw", "w_planes_raw")
+        load_rows(w2_raw[0], w2, 0)
+        load_rows(w2_raw[1], w2, 1)
+        nc.sync.dma_start(out=w3_raw[:], in_=w3_words.rearrange("a p c i -> p a (c i)").bitcast(I32))
+        round_w2(0)
+        quantize_w2(0)
+        round_w2(1)
+        quantize_w2(1)
+        deal(w3_codes[:], w3_raw[:])
+        w3_planes = held([P, H], U8, "w3_planes")
+        nc.vector.tensor_copy(
+            out=w3_planes[:].rearrange("p (t m) -> p m t", t=PACK), in_=w3_planes_raw[:].rearrange("p (m t) -> p m t", t=PACK)
+        )
+
+        w5_raw = [held([P, PACK, N], F32, f"w5_raw{a}", ("tab1", "tab_planes")[a]) for a in range(PASSES)]
+        w4_raw = held([P, PACK, N], F32, "w4_raw", "tab0")
+        bias = held([P, N // P], F32, "bias", "w1_raw")
+        load_rows(w5_raw[0], w5, 0)
+        with nc.allow_non_contiguous_dma(reason="one bias value a partition"):
+            nc.sync.dma_start(out=bias[:], in_=b5.rearrange("(c p) -> p c", p=P))
+        load_rows(w5_raw[1], w5, 1)
+        load_rows(w4_raw, w4, 0)
+
+        def product(tag, s, codes, planes, v_plane=lambda a: v_planes[4 * a : P]):
+            acc = psum.tile([P, HALF], F32, name="acc", tag=tag)
+            for a in range(PASSES):
+                nc.tensor.matmul_mx(
+                    out=acc[:], lhsT=codes(a), lhsT_scale=planes(a),
+                    rhs=v_words[a][s][:].bitcast(FP8X4), rhs_scale=v_plane(a)[:, s * HALF : (s + 1) * HALF],
+                    start=(a == 0), stop=(a == PASSES - 1),
+                )
+            return acc
+
+        h_rows = [held([P, PACK, HALF], F32, f"h_rows{s}") for s in range(HALVES)]
+        h_bf = [held([P, HALF, PACK], BF16, f"h_bf{s}") for s in range(HALVES)]
+        h_codes = held([P, S], U32, "h_codes")
+        h_plane = held([P, S], U8, "h_plane")
+
+        w5_bf = [held([P, PASSES, CHUNK, PACK], BF16, f"w5_bf{u}") for u in range(CHUNKS)]
+        w5_codes = [held([P, PASSES, CHUNK], U32, f"w5_codes{u}") for u in range(CHUNKS)]
+        w5_planes = [held([P, PASSES, CHUNK], U8, f"w5_planes{u}") for u in range(CHUNKS)]
+        w4_bf = [held([P, CHUNK, PACK], BF16, f"w4_bf{u}") for u in range(CHUNKS)]
+        w4_codes = [held([P, CHUNK], U32, f"w4_codes{u}") for u in range(CHUNKS)]
+        w4_planes = [held([P, CHUNK], U8, f"w4_planes{u}") for u in range(CHUNKS)]
+
+        def round_w5(a, u):
+            interleave(nc, W5_ENGINES[a][u], w5_bf[u][:, a], w5_raw[a][:, :, u * CHUNK : (u + 1) * CHUNK])
+
+        def quantize_w5(u):
+            quantize(
+                nc, w5_codes[u][:].rearrange("p a c -> p (a c)"), w5_planes[u][:].rearrange("p a c -> p (a c)"),
+                w5_bf[u][:].rearrange("p a c j -> p (a c j)"),
+            )
+
+        def round_w4(u):
+            interleave(nc, W4_ENGINES[u], w4_bf[u][:], w4_raw[:, :, u * CHUNK : (u + 1) * CHUNK])
+
+        def quantize_w4(u):
+            quantize(nc, w4_codes[u][:], w4_planes[u][:], w4_bf[u][:].rearrange("p c j -> p (c j)"))
+
+        def first_factor(s, t):
+            cols = slice(t * P, (t + 1) * P)
+            acc_a = product("ae"[t % 2], s, lambda a: w1_codes[:, a, 2 * t * P : 2 * (t + 1) * P].bitcast(FP4X4),
+                            lambda a: w_planes[:, a, cols], lambda a: (v_planes, v_plane1)[a][:])
+            first = ring.tile([P, HALF], F32, name="first", bufs=8)
+            nc.scalar.copy(out=first[:], in_=acc_a[:])
+            return first
+
+        def h_first(s, t):
+            cols = slice(t * P, (t + 1) * P)
+            first = firsts[s, t]
+            acc_b = product("b", s, lambda a: w2_codes[a][:, cols].bitcast(FP8X4), lambda a: w2_planes[a][:, cols])
+            acc_c = product("c", s, lambda a: w3_codes[:, a, cols].bitcast(FP8X4), lambda a: w3_planes[4 * a : P, cols])
+            both = ring.tile([P, HALF], F32, name="both")
+            nc.vector.tensor_tensor(out=both[:], in0=acc_b[:], in1=first[:], op=ALU.mult)
+            return both, acc_c
+
+        def h_second(s, t, both, acc_c):
+            nc.vector.tensor_tensor(out=h_rows[s][:, t, :], in0=acc_c[:], in1=both[:], op=ALU.add)
+
+        def round_h(s):
+            width = HALF // len(H_ENGINES[s])
+            for part, engine in enumerate(H_ENGINES[s]):
+                cols = slice(part * width, (part + 1) * width)
+                interleave(nc, engine, h_bf[s][:, cols, :], h_rows[s][:, :, cols])
+
+        def quantize_h(s):
+            cols = slice(s * HALF, (s + 1) * HALF)
+            quantize(nc, h_codes[:, cols], h_plane[:, cols], h_bf[s][:].rearrange("p c j -> p (c j)"))
+
+        def store_h(s, ts):
+            cols = slice(s * HALF, (s + 1) * HALF)
+            nc.sync.dma_start(out=out_1[:, cols].rearrange("(p t) c -> p t c", t=PACK)[:, ts], in_=h_rows[s][:, ts])
+
+        tiles = N // P
+        y_rows = [held([P, S], F32, f"y_rows{c}") for c in range(tiles)]
+
+        def estimate(c, s):
+            u, cols = c // 2, slice((c % 2) * P, (c % 2 + 1) * P)
+            acc_e = product("ea"[c % 2], s, lambda a: w5_codes[u][:, a, cols].bitcast(FP8X4),
+                            lambda a: w5_planes[u][:, a, cols])
+            gate = held([P, HALF], F32, f"gate{c}{s}")
+            nc.scalar.activation(out=gate[:], in_=acc_e[:], func=ACT.Silu, bias=bias[:, c : c + 1])
+            return gate
+
+        def repair(c, s, gate):
+            u, cols = c // 2, slice((c % 2) * P, (c % 2 + 1) * P)
+            js = slice(s * HALF, (s + 1) * HALF)
+            acc_y = psum.tile([P, HALF], F32, name="acc", tag="bc"[c % 2])
+            nc.tensor.matmul_mx(
+                out=acc_y[:], lhsT=w4_codes[u][:, cols].bitcast(FP8X4), lhsT_scale=w4_planes[u][:, cols],
+                rhs=h_codes[:, js].bitcast(FP8X4), rhs_scale=h_plane[:, js], start=True, stop=True,
+            )
+            nc.vector.tensor_tensor(out=y_rows[c][:, js], in0=acc_y[:], in1=gate[:], op=ALU.subtract)
+
+        def store_planes():
+            nc.sync.dma_start(out=out_2[0].rearrange("p m t -> p (m t)").bitcast(I32), in_=h_codes[:].bitcast(I32))
+            for q in range(4):
+                nc.sync.dma_start(
+                    out=out_3[0, 4 * q : 4 * q + 4, :].bitcast(I32), in_=h_plane[32 * q : 32 * q + 4, :].bitcast(I32)
+                )
+
+        def store_y(c, js):
+            nc.sync.dma_start(out=out_0[c * P : (c + 1) * P, js], in_=y_rows[c][:, js])
+
+        steps = [(s, t) for s in range(HALVES) for t in range(PACK)]
+        firsts = {step: first_factor(*step) for step in steps}
+        gates = {}
+        pending = None
+
+        def finish(s, t, both, acc_c):
+            h_second(s, t, both, acc_c)
+            if t % 2 == 1:
+                store_h(s, slice(t - 1, t + 1))
+            if t == PACK - 1:
+                round_h(s)
+
+        for u in range(CHUNKS):
+            round_w5(0, u)
+        for i, (s, t) in enumerate(steps):
+            made = h_first(s, t)
+            if pending is not None:
+                finish(*pending)
+            pending = (s, t) + made
+            if 4 <= i <= 6:
+                round_w5(1, i - 4)
+                quantize_w5(i - 4)
+            if i == 5:
+                quantize_h(0)
+        finish(*pending)
+        for u in range(CHUNKS):
+            round_w4(u)
+            quantize_w4(u)
+            for c in (2 * u, 2 * u + 1):
+                gates[c, 0] = estimate(c, 0)
+        quantize_h(1)
+        store_planes()
+        for s in range(HALVES):
+            for c in range(tiles):
+                if s == 0:
+                    gates[c, 1] = estimate(c, 1)
+                repair(c, s, gates[c, s])
+                store_y(c, slice(s * HALF, (s + 1) * HALF))

@@ -1,6 +1,7 @@
 from contextlib import ExitStack
 
 import concourse.mybir as mybir
+from concourse.masks import make_identity
 
 K, H, N, T, S = 1024, 512, 768, 2048, 1024
 FLOPS = 2 * S * (3 * K * H + K * N + H * N)
@@ -24,10 +25,10 @@ HALVES = S // HALF
 CHUNK = 256
 CHUNKS = N // CHUNK
 
-W5_ENGINES = (("s", "s", "s"), ("s", "s", "s"))
-W4_ENGINES = ("s", "s", "s")
-H_ENGINES = (("s","v"), ("s","v"))
-W2_ENGINES = (("v",), ("v",))
+W5_ENGINES = (("s", "s", "g"), ("s", "g", "g"))
+W4_ENGINES = ("s", "g", "s")
+H_ENGINES = (("s","s"), ("s","s"))
+W2_ENGINES = (("s",), ("v",))
 
 
 def cast(nc, engine, out, in_):
@@ -41,7 +42,10 @@ def cast(nc, engine, out, in_):
 
 def interleave(nc, engine, grouped, rows):
     if engine == "g":
-        cast(nc, engine, grouped, rows.rearrange("p j c -> p c j"))
+        width = grouped.shape[1] // 2
+        for part in range(2):
+            cols = slice(part * width, (part + 1) * width)
+            cast(nc, engine, grouped[:, cols, :], rows[:, :, cols].rearrange("p j c -> p c j"))
         return
     cast(
         nc,
@@ -114,8 +118,20 @@ def tile_list_chirp_interference_repair_kernel(
             )
         load_tab(0)
         load_planes(nc.sync, w_planes_raw, 0, w1_scales)
+        w2_raw = [held([P, PACK, H], F32, "w2_raw0")]
+        load_rows(w2_raw[0], w2, 0)
         load_tab(1)
         load_packed(w3_planes_raw, w3_scales)
+
+        bias_rows = held([P, P], F32, "bias_rows")
+        identity = held([P, P], F32, "identity")
+        bias = held([P, N // P], F32, "bias")
+        nc.gpsimd.memset(bias_rows[:], 0.0)
+        nc.gpsimd.dma_start(out=bias_rows[0 : N // P, :], in_=b5.rearrange("(c p) -> c p", p=P))
+        make_identity(nc, identity[:])
+        bias_t = psum.tile([P, HALF], F32, name="acc", tag="c")
+        nc.tensor.transpose(bias_t[:, 0:P], bias_rows[:], identity[:])
+        nc.scalar.copy(out=bias[:], in_=bias_t[:, 0 : N // P])
 
         v_words = [[held([P, HALF], U32, f"v_words{a}{s}") for s in range(HALVES)] for a in range(PASSES)]
 
@@ -160,16 +176,15 @@ def tile_list_chirp_interference_repair_kernel(
         gather_planes()
         gather_words(0, 0)
         deal(w_planes[:], w_planes_raw[:])
-        gather_words(1, 0)
         gather_words(0, 1)
-        gather_words(1, 1)
-        w2_raw = [held([P, PACK, H], F32, f"w2_raw{a}", ("tab_planes", "tab0")[a]) for a in range(PASSES)]
+        w2_raw.append(held([P, PACK, H], F32, "w2_raw1", "tab_planes"))
         w3_raw = held([P, PASSES, H], I32, "w3_raw", "w_planes_raw")
-        load_rows(w2_raw[0], w2, 0)
         load_rows(w2_raw[1], w2, 1)
         nc.sync.dma_start(out=w3_raw[:], in_=w3_words.rearrange("a p c i -> p a (c i)").bitcast(I32))
         round_w2(0)
         quantize_w2(0)
+        gather_words(1, 0)
+        gather_words(1, 1)
         round_w2(1)
         quantize_w2(1)
         deal(w3_codes[:], w3_raw[:])
@@ -178,12 +193,9 @@ def tile_list_chirp_interference_repair_kernel(
             out=w3_planes[:].rearrange("p (t m) -> p m t", t=PACK), in_=w3_planes_raw[:].rearrange("p (m t) -> p m t", t=PACK)
         )
 
-        w5_raw = [held([P, PACK, N], F32, f"w5_raw{a}", ("tab1", "tab_planes")[a]) for a in range(PASSES)]
-        w4_raw = held([P, PACK, N], F32, "w4_raw", "tab0")
-        bias = held([P, N // P], F32, "bias", "w1_raw")
+        w5_raw = [held([P, PACK, N], F32, f"w5_raw{a}", ("tab0", "w2_raw0")[a]) for a in range(PASSES)]
+        w4_raw = held([P, PACK, N], F32, "w4_raw", "tab1")
         load_rows(w5_raw[0], w5, 0)
-        with nc.allow_non_contiguous_dma(reason="one bias value a partition"):
-            nc.sync.dma_start(out=bias[:], in_=b5.rearrange("(c p) -> p c", p=P))
         load_rows(w5_raw[1], w5, 1)
         load_rows(w4_raw, w4, 0)
 

@@ -25,9 +25,9 @@ HALVES = S // HALF
 CHUNK = 256
 CHUNKS = N // CHUNK
 
-W5_ENGINES = (("s", "s", "g"), ("s", "g", "g"))
-W4_ENGINES = ("s", "g", "s")
-H_ENGINES = (("s","s"), ("s","s"))
+W5_ENGINES = (("s", "s", "s"), ("s", "s", "s"))
+W4_ENGINES = ("s", "s", "s")
+H_ENGINES = (("v",), ("s","v"))
 W2_ENGINES = (("s",), ("v",))
 
 
@@ -79,8 +79,6 @@ def tile_list_chirp_interference_repair_kernel(
         w_planes_raw = held([P, PASSES, H], U8, "w_planes_raw")
         nc.vector.memset(tab_planes[:].bitcast(I32), 0)
         nc.gpsimd.memset(w_planes_raw[:].bitcast(I32), 0)
-        w3_planes_raw = held([P, H], U8, "w3_planes_raw")
-        nc.gpsimd.memset(w3_planes_raw[:].bitcast(I32), 0)
         nc.gpsimd.memset(v_plane1[:].bitcast(I32), 0)
 
         warm = held([P, 8], F32, "warm")
@@ -121,7 +119,6 @@ def tile_list_chirp_interference_repair_kernel(
         w2_raw = [held([P, PACK, H], F32, "w2_raw0")]
         load_rows(w2_raw[0], w2, 0)
         load_tab(1)
-        load_packed(w3_planes_raw, w3_scales)
 
         bias_rows = held([P, P], F32, "bias_rows")
         identity = held([P, P], F32, "identity")
@@ -178,8 +175,11 @@ def tile_list_chirp_interference_repair_kernel(
         deal(w_planes[:], w_planes_raw[:])
         gather_words(0, 1)
         w2_raw.append(held([P, PACK, H], F32, "w2_raw1", "tab_planes"))
-        w3_raw = held([P, PASSES, H], I32, "w3_raw", "w_planes_raw")
+        w3_planes_raw = held([P, H], U8, "w3_planes_raw", "w_planes_raw")
+        nc.gpsimd.memset(w3_planes_raw[:].bitcast(I32), 0)
+        w3_raw = held([P, PASSES, H], I32, "w3_raw", "tab0")
         load_rows(w2_raw[1], w2, 1)
+        load_packed(w3_planes_raw, w3_scales)
         nc.sync.dma_start(out=w3_raw[:], in_=w3_words.rearrange("a p c i -> p a (c i)").bitcast(I32))
         round_w2(0)
         quantize_w2(0)
@@ -193,8 +193,8 @@ def tile_list_chirp_interference_repair_kernel(
             out=w3_planes[:].rearrange("p (t m) -> p m t", t=PACK), in_=w3_planes_raw[:].rearrange("p (m t) -> p m t", t=PACK)
         )
 
-        w5_raw = [held([P, PACK, N], F32, f"w5_raw{a}", ("tab0", "w2_raw0")[a]) for a in range(PASSES)]
-        w4_raw = held([P, PACK, N], F32, "w4_raw", "tab1")
+        w5_raw = [held([P, PACK, N], F32, f"w5_raw{a}", ("w2_raw0", "tab1")[a]) for a in range(PASSES)]
+        w4_raw = held([P, PACK, N], F32, "w4_raw", "tab_planes")
         load_rows(w5_raw[0], w5, 0)
         load_rows(w5_raw[1], w5, 1)
         load_rows(w4_raw, w4, 0)
@@ -265,6 +265,9 @@ def tile_list_chirp_interference_repair_kernel(
         def quantize_h(s):
             cols = slice(s * HALF, (s + 1) * HALF)
             quantize(nc, h_codes[:, cols], h_plane[:, cols], h_bf[s][:].rearrange("p c j -> p (c j)"))
+            nc.sync.dma_start(
+                out=out_2[0].rearrange("p m t -> p (m t)").bitcast(I32)[:, cols], in_=h_codes[:, cols].bitcast(I32)
+            )
 
         def store_h(s, ts):
             cols = slice(s * HALF, (s + 1) * HALF)
@@ -289,10 +292,23 @@ def tile_list_chirp_interference_repair_kernel(
                 out=acc_y[:], lhsT=w4_codes[u][:, cols].bitcast(FP8X4), lhsT_scale=w4_planes[u][:, cols],
                 rhs=h_codes[:, js].bitcast(FP8X4), rhs_scale=h_plane[:, js], start=True, stop=True,
             )
-            nc.vector.tensor_tensor(out=y_rows[c][:, js], in0=acc_y[:], in1=gate[:], op=ALU.subtract)
+            if (c, s) in ():
+                product_rows = ring.tile([P, HALF], F32, name="product_rows")
+                nc.scalar.copy(out=product_rows[:], in_=acc_y[:])
+                nc.gpsimd.tensor_tensor(out=y_rows[c][:, js], in0=product_rows[:], in1=gate[:], op=ALU.subtract)
+                store_y(c, js)
+            else:
+                parts = 2 if (c, s) == (tiles - 1, HALVES - 1) else 1
+                width = HALF // parts
+                for part in range(parts):
+                    inner = slice(part * width, (part + 1) * width)
+                    outer = slice(s * HALF + part * width, s * HALF + (part + 1) * width)
+                    nc.vector.tensor_tensor(
+                        out=y_rows[c][:, outer], in0=acc_y[:, inner], in1=gate[:, inner], op=ALU.subtract
+                    )
+                    store_y(c, outer)
 
         def store_planes():
-            nc.sync.dma_start(out=out_2[0].rearrange("p m t -> p (m t)").bitcast(I32), in_=h_codes[:].bitcast(I32))
             for q in range(4):
                 nc.sync.dma_start(
                     out=out_3[0, 4 * q : 4 * q + 4, :].bitcast(I32), in_=h_plane[32 * q : 32 * q + 4, :].bitcast(I32)
@@ -310,7 +326,7 @@ def tile_list_chirp_interference_repair_kernel(
             h_second(s, t, both, acc_c)
             if t % 2 == 1:
                 store_h(s, slice(t - 1, t + 1))
-            if t == PACK - 1:
+            if (s, t) == (0, PACK - 1):
                 round_h(s)
 
         for u in range(CHUNKS):
@@ -331,11 +347,13 @@ def tile_list_chirp_interference_repair_kernel(
             quantize_w4(u)
             for c in (2 * u, 2 * u + 1):
                 gates[c, 0] = estimate(c, 0)
-        quantize_h(1)
-        store_planes()
         for s in range(HALVES):
             for c in range(tiles):
+                if (s, c) == (0, 1):
+                    round_h(1)
+                if (s, c) == (0, 3):
+                    quantize_h(1)
+                    store_planes()
                 if s == 0:
                     gates[c, 1] = estimate(c, 1)
                 repair(c, s, gates[c, s])
-                store_y(c, slice(s * HALF, (s + 1) * HALF))

from contextlib import ExitStack

import concourse.mybir as mybir
from concourse.masks import make_identity

K, H, N, T, S = 1024, 512, 768, 2048, 1024
FLOPS = 2 * S * (3 * K * H + K * N + H * N)

F32 = mybir.dt.float32
BF16 = mybir.dt.bfloat16
I32 = mybir.dt.int32
U32 = mybir.dt.uint32
U16 = mybir.dt.uint16
U8 = mybir.dt.uint8
FP8X4 = mybir.dt.float8_e4m3fn_x4
FP4X4 = mybir.dt.float4_e2m1fn_x4
ALU = mybir.AluOpType
ACT = mybir.ActivationFunctionType

P = 128
PACK = 4
PASSES = K // (P * PACK)
HALF = 512
HALVES = S // HALF
CHUNK = 256
CHUNKS = N // CHUNK

W5_ENGINES = (("s", "s", "s"), ("s", "s", "s"))
W4_ENGINES = ("s", "s", "s")
H_ENGINES = (("v",), ("s","v"))
W2_ENGINES = (("s",), ("v",))


def cast(nc, engine, out, in_):
    if engine == "v":
        nc.vector.tensor_copy(out=out, in_=in_)
    elif engine == "s":
        nc.scalar.copy(out=out, in_=in_)
    else:
        nc.gpsimd.tensor_scalar(out=out, in0=in_, scalar1=1.0, scalar2=0.0, op0=ALU.mult, op1=ALU.add)


def interleave(nc, engine, grouped, rows):
    if engine == "g":
        width = grouped.shape[1] // 2
        for part in range(2):
            cols = slice(part * width, (part + 1) * width)
            cast(nc, engine, grouped[:, cols, :], rows[:, :, cols].rearrange("p j c -> p c j"))
        return
    cast(
        nc,
        engine,
        grouped.rearrange("p (c i) j -> p c j i", i=4),
        rows.rearrange("p j (c i) -> p c j i", i=4),
    )


def quantize(nc, codes, scales, grouped):
    nc.vector.quantize_mx(out=codes.bitcast(FP8X4), scales=scales, in_=grouped)


def tile_list_chirp_interference_repair_kernel(
    tc, tab_words, tab_scales, offs, w1_words, w1_scales, w2, w3_words, w3_scales, w4, w5, b5,
    out_0, out_1, out_2, out_3,
):
    nc = tc.nc
    with ExitStack() as ctx:
        keep = ctx.enter_context(tc.tile_pool(name="keep", bufs=1))
        ring = ctx.enter_context(tc.tile_pool(name="ring", bufs=3))
        psum = ctx.enter_context(tc.psum_pool(name="psum", bufs=2))

        def held(shape, dtype, name, tag=""):
            return keep.tile(shape, dtype, name=name, tag=tag or name, align_bytes=64)

        offsets = keep.tile([P, S // 16], U16, name="offsets")
        tab_planes = held([P, T], U8, "tab_planes")
        v_planes = held([P, S], U8, "v_planes")
        v_plane1 = held([P, S], U8, "v_plane1")
        w_planes_raw = held([P, PASSES, H], U8, "w_planes_raw")
        nc.vector.memset(tab_planes[:].bitcast(I32), 0)
        nc.gpsimd.memset(w_planes_raw[:].bitcast(I32), 0)
        nc.gpsimd.memset(v_plane1[:].bitcast(I32), 0)

        warm = held([P, 8], F32, "warm")
        nc.gpsimd.memset(warm[:, 0:1], 0.0)
        nc.scalar.activation(out=warm[:, 1:2], in_=warm[:, 0:1], func=ACT.Silu)

        w1_raw = held([P, PASSES, 2 * H], U8, "w1_raw")
        tab = [held([P, T], I32, f"tab{a}") for a in range(PASSES)]

        def load_rows(tile, w, a):
            nc.sync.dma_start(out=tile[:], in_=w[512 * a : 512 * (a + 1), :].rearrange("(p j) c -> p j c", j=PACK))

        def load_tab(a):
            nc.sync.dma_start(out=tab[a][:], in_=tab_words[a].rearrange("p t i -> p (t i)").bitcast(I32))

        def load_packed(tile, scales):
            for q in range(4):
                nc.sync.dma_start(
                    out=tile[32 * q : 32 * q + 8, :].bitcast(I32), in_=scales[:, 4 * q : 4 * q + 4, :].bitcast(I32)
                )

        def load_planes(queue, tile, first, scales):
            for q in range(4):
                queue.dma_start(
                    out=tile[32 * q + first : 32 * q + first + 4].bitcast(I32),
                    in_=scales[:, 4 * q : 4 * q + 4, :].rearrange("a r c -> r a c").bitcast(I32),
                )

        nc.sync.dma_start(out=w1_raw[:].bitcast(I32), in_=w1_words.rearrange("a p c -> p a c").bitcast(I32))
        nc.sync.dma_start(offsets[:], offs)
        for q in range(4):
            nc.sync.dma_start(
                out=tab_planes[32 * q : 32 * q + 8, :].bitcast(I32),
                in_=tab_scales[:, 4 * q : 4 * q + 4, :].bitcast(I32),
            )
        load_tab(0)
        load_planes(nc.sync, w_planes_raw, 0, w1_scales)
        w2_raw = [held([P, PACK, H], F32, "w2_raw0")]
        load_rows(w2_raw[0], w2, 0)
        load_tab(1)

        bias_rows = held([P, P], F32, "bias_rows")
        identity = held([P, P], F32, "identity")
        bias = held([P, N // P], F32, "bias")
        nc.gpsimd.memset(bias_rows[:], 0.0)
        nc.gpsimd.dma_start(out=bias_rows[0 : N // P, :], in_=b5.rearrange("(c p) -> c p", p=P))
        make_identity(nc, identity[:])
        bias_t = psum.tile([P, HALF], F32, name="acc", tag="c")
        nc.tensor.transpose(bias_t[:, 0:P], bias_rows[:], identity[:])
        nc.scalar.copy(out=bias[:], in_=bias_t[:, 0 : N // P])

        v_words = [[held([P, HALF], U32, f"v_words{a}{s}") for s in range(HALVES)] for a in range(PASSES)]

        def picks(s):
            return offsets[:, s * HALF // 16 : (s + 1) * HALF // 16]

        def gather_words(a, s):
            nc.vector.tensor_copy(v_words[a][s][:], tab[a][:].bitcast(U32).indirect(picks(s)))

        def gather_planes():
            nc.vector.tensor_copy(v_planes[:], tab_planes[:].indirect(offsets[:]))
            nc.scalar.dma_start(out=v_plane1[0:100, :].bitcast(I32), in_=v_planes[4:104, :].bitcast(I32))

        w1_codes = held([P, PASSES, 2 * H], U8, "w1_codes")
        w3_codes = held([P, PASSES, H], I32, "w3_codes")
        w_planes = held([P, PASSES, H], U8, "w_planes")

        def deal(out, in_):
            nc.vector.tensor_copy(
                out=out.rearrange("p a (t m) -> p a m t", t=PACK), in_=in_.rearrange("p a (m t) -> p a m t", t=PACK)
            )

        w2_bf = [held([P, PACK, P, PACK], BF16, f"w2_bf{a}") for a in range(PASSES)]
        w2_codes = [held([P, H], U32, f"w2_codes{a}") for a in range(PASSES)]
        w2_planes = [held([P, H], U8, f"w2_planes{a}") for a in range(PASSES)]

        def round_w2(a):
            for part, engine in enumerate(W2_ENGINES[a]):
                width = P // len(W2_ENGINES[a])
                ms = slice(part * width, (part + 1) * width)
                cast(
                    nc,
                    engine,
                    w2_bf[a][:, :, ms, :].rearrange("p t m j -> p m j t"),
                    w2_raw[a][:].rearrange("p j (m t) -> p m j t", t=PACK)[:, ms],
                )

        def quantize_w2(a):
            quantize(nc, w2_codes[a][:], w2_planes[a][:], w2_bf[a][:].rearrange("p t m j -> p (t m j)"))

        deal(w1_codes[:].bitcast(U16), w1_raw[:].bitcast(U16))
        gather_planes()
        gather_words(0, 0)
        deal(w_planes[:], w_planes_raw[:])
        gather_words(0, 1)
        w2_raw.append(held([P, PACK, H], F32, "w2_raw1", "tab_planes"))
        w3_planes_raw = held([P, H], U8, "w3_planes_raw", "w_planes_raw")
        nc.gpsimd.memset(w3_planes_raw[:].bitcast(I32), 0)
        w3_raw = held([P, PASSES, H], I32, "w3_raw", "tab0")
        load_rows(w2_raw[1], w2, 1)
        load_packed(w3_planes_raw, w3_scales)
        nc.sync.dma_start(out=w3_raw[:], in_=w3_words.rearrange("a p c i -> p a (c i)").bitcast(I32))
        round_w2(0)
        quantize_w2(0)
        gather_words(1, 0)
        gather_words(1, 1)
        round_w2(1)
        quantize_w2(1)
        deal(w3_codes[:], w3_raw[:])
        w3_planes = held([P, H], U8, "w3_planes")
        nc.vector.tensor_copy(
            out=w3_planes[:].rearrange("p (t m) -> p m t", t=PACK), in_=w3_planes_raw[:].rearrange("p (m t) -> p m t", t=PACK)
        )

        w5_raw = [held([P, PACK, N], F32, f"w5_raw{a}", ("w2_raw0", "tab1")[a]) for a in range(PASSES)]
        w4_raw = held([P, PACK, N], F32, "w4_raw", "tab_planes")
        load_rows(w5_raw[0], w5, 0)
        load_rows(w5_raw[1], w5, 1)
        load_rows(w4_raw, w4, 0)

        def product(tag, s, codes, planes, v_plane=lambda a: v_planes[4 * a : P]):
            acc = psum.tile([P, HALF], F32, name="acc", tag=tag)
            for a in range(PASSES):
                nc.tensor.matmul_mx(
                    out=acc[:], lhsT=codes(a), lhsT_scale=planes(a),
                    rhs=v_words[a][s][:].bitcast(FP8X4), rhs_scale=v_plane(a)[:, s * HALF : (s + 1) * HALF],
                    start=(a == 0), stop=(a == PASSES - 1),
                )
            return acc

        h_rows = [held([P, PACK, HALF], F32, f"h_rows{s}") for s in range(HALVES)]
        h_bf = [held([P, HALF, PACK], BF16, f"h_bf{s}") for s in range(HALVES)]
        h_codes = held([P, S], U32, "h_codes")
        h_plane = held([P, S], U8, "h_plane")

        w5_bf = [held([P, PASSES, CHUNK, PACK], BF16, f"w5_bf{u}") for u in range(CHUNKS)]
        w5_codes = [held([P, PASSES, CHUNK], U32, f"w5_codes{u}") for u in range(CHUNKS)]
        w5_planes = [held([P, PASSES, CHUNK], U8, f"w5_planes{u}") for u in range(CHUNKS)]
        w4_bf = [held([P, CHUNK, PACK], BF16, f"w4_bf{u}") for u in range(CHUNKS)]
        w4_codes = [held([P, CHUNK], U32, f"w4_codes{u}") for u in range(CHUNKS)]
        w4_planes = [held([P, CHUNK], U8, f"w4_planes{u}") for u in range(CHUNKS)]

        def round_w5(a, u):
            interleave(nc, W5_ENGINES[a][u], w5_bf[u][:, a], w5_raw[a][:, :, u * CHUNK : (u + 1) * CHUNK])

        def quantize_w5(u):
            quantize(
                nc, w5_codes[u][:].rearrange("p a c -> p (a c)"), w5_planes[u][:].rearrange("p a c -> p (a c)"),
                w5_bf[u][:].rearrange("p a c j -> p (a c j)"),
            )

        def round_w4(u):
            interleave(nc, W4_ENGINES[u], w4_bf[u][:], w4_raw[:, :, u * CHUNK : (u + 1) * CHUNK])

        def quantize_w4(u):
            quantize(nc, w4_codes[u][:], w4_planes[u][:], w4_bf[u][:].rearrange("p c j -> p (c j)"))

        def first_factor(s, t):
            cols = slice(t * P, (t + 1) * P)
            acc_a = product("ae"[t % 2], s, lambda a: w1_codes[:, a, 2 * t * P : 2 * (t + 1) * P].bitcast(FP4X4),
                            lambda a: w_planes[:, a, cols], lambda a: (v_planes, v_plane1)[a][:])
            first = ring.tile([P, HALF], F32, name="first", bufs=8)
            nc.scalar.copy(out=first[:], in_=acc_a[:])
            return first

        def h_first(s, t):
            cols = slice(t * P, (t + 1) * P)
            first = firsts[s, t]
            acc_b = product("b", s, lambda a: w2_codes[a][:, cols].bitcast(FP8X4), lambda a: w2_planes[a][:, cols])
            acc_c = product("c", s, lambda a: w3_codes[:, a, cols].bitcast(FP8X4), lambda a: w3_planes[4 * a : P, cols])
            both = ring.tile([P, HALF], F32, name="both")
            nc.vector.tensor_tensor(out=both[:], in0=acc_b[:], in1=first[:], op=ALU.mult)
            return both, acc_c

        def h_second(s, t, both, acc_c):
            nc.vector.tensor_tensor(out=h_rows[s][:, t, :], in0=acc_c[:], in1=both[:], op=ALU.add)

        def round_h(s):
            width = HALF // len(H_ENGINES[s])
            for part, engine in enumerate(H_ENGINES[s]):
                cols = slice(part * width, (part + 1) * width)
                interleave(nc, engine, h_bf[s][:, cols, :], h_rows[s][:, :, cols])

        def quantize_h(s):
            cols = slice(s * HALF, (s + 1) * HALF)
            quantize(nc, h_codes[:, cols], h_plane[:, cols], h_bf[s][:].rearrange("p c j -> p (c j)"))
            nc.sync.dma_start(
                out=out_2[0].rearrange("p m t -> p (m t)").bitcast(I32)[:, cols], in_=h_codes[:, cols].bitcast(I32)
            )

        def store_h(s, ts):
            cols = slice(s * HALF, (s + 1) * HALF)
            nc.sync.dma_start(out=out_1[:, cols].rearrange("(p t) c -> p t c", t=PACK)[:, ts], in_=h_rows[s][:, ts])

        tiles = N // P
        y_rows = [held([P, S], F32, f"y_rows{c}") for c in range(tiles)]

        def estimate(c, s):
            u, cols = c // 2, slice((c % 2) * P, (c % 2 + 1) * P)
            acc_e = product("ea"[c % 2], s, lambda a: w5_codes[u][:, a, cols].bitcast(FP8X4),
                            lambda a: w5_planes[u][:, a, cols])
            gate = held([P, HALF], F32, f"gate{c}{s}")
            nc.scalar.activation(out=gate[:], in_=acc_e[:], func=ACT.Silu, bias=bias[:, c : c + 1])
            return gate

        def repair(c, s, gate):
            u, cols = c // 2, slice((c % 2) * P, (c % 2 + 1) * P)
            js = slice(s * HALF, (s + 1) * HALF)
            acc_y = psum.tile([P, HALF], F32, name="acc", tag="bc"[c % 2])
            nc.tensor.matmul_mx(
                out=acc_y[:], lhsT=w4_codes[u][:, cols].bitcast(FP8X4), lhsT_scale=w4_planes[u][:, cols],
                rhs=h_codes[:, js].bitcast(FP8X4), rhs_scale=h_plane[:, js], start=True, stop=True,
            )
            if (c, s) in ():
                product_rows = ring.tile([P, HALF], F32, name="product_rows")
                nc.scalar.copy(out=product_rows[:], in_=acc_y[:])
                nc.gpsimd.tensor_tensor(out=y_rows[c][:, js], in0=product_rows[:], in1=gate[:], op=ALU.subtract)
                store_y(c, js)
            else:
                parts = 2 if (c, s) == (tiles - 1, HALVES - 1) else 1
                width = HALF // parts
                for part in range(parts):
                    inner = slice(part * width, (part + 1) * width)
                    outer = slice(s * HALF + part * width, s * HALF + (part + 1) * width)
                    nc.vector.tensor_tensor(
                        out=y_rows[c][:, outer], in0=acc_y[:, inner], in1=gate[:, inner], op=ALU.subtract
                    )
                    store_y(c, outer)

        def store_planes():
            for q in range(4):
                nc.sync.dma_start(
                    out=out_3[0, 4 * q : 4 * q + 4, :].bitcast(I32), in_=h_plane[32 * q : 32 * q + 4, :].bitcast(I32)
                )

        def store_y(c, js):
            nc.sync.dma_start(out=out_0[c * P : (c + 1) * P, js], in_=y_rows[c][:, js])

        steps = [(s, t) for s in range(HALVES) for t in range(PACK)]
        firsts = {step: first_factor(*step) for step in steps}
        gates = {}
        pending = None

        def finish(s, t, both, acc_c):
            h_second(s, t, both, acc_c)
            if t % 2 == 1:
                store_h(s, slice(t - 1, t + 1))
            if (s, t) == (0, PACK - 1):
                round_h(s)

        for u in range(CHUNKS):
            round_w5(0, u)
        for i, (s, t) in enumerate(steps):
            made = h_first(s, t)
            if pending is not None:
                finish(*pending)
            pending = (s, t) + made
            if 4 <= i <= 6:
                round_w5(1, i - 4)
                quantize_w5(i - 4)
            if i == 5:
                quantize_h(0)
        finish(*pending)
        for u in range(CHUNKS):
            round_w4(u)
            quantize_w4(u)
            for c in (2 * u, 2 * u + 1):
                gates[c, 0] = estimate(c, 0)
        for s in range(HALVES):
            for c in range(tiles):
                if (s, c) == (0, 1):
                    round_h(1)
                if (s, c) == (0, 3):
                    quantize_h(1)
                    store_planes()
                if s == 0:
                    gates[c, 1] = estimate(c, 1)
                repair(c, s, gates[c, s])
